import numpy as np
import ml_dtypes


def mxq(x, axis, fmt="e4m3"):
    dtype, down = {"e4m3": (ml_dtypes.float8_e4m3fn, 7), "e5m2": (ml_dtypes.float8_e5m2, 14)}[fmt]
    v = np.moveaxis(np.asarray(x, np.float32).astype(ml_dtypes.bfloat16).astype(np.float64), axis, -1)
    blocks = v.reshape(v.shape[:-1] + (-1, 32))
    amax = np.abs(blocks).max(-1, keepdims=True)
    byte = np.maximum(np.where(amax > 0, np.frexp(amax)[1] - 1 + 127, 0) - down, 1)
    scale = np.exp2(byte - 127.0)
    codes = (blocks / scale).astype(np.float32).astype(dtype).astype(np.float64)
    return np.moveaxis((codes * scale).reshape(v.shape), -1, axis)


WIDE = False


def mx_kscale(k):
    if not WIDE:
        return np.ones(k)
    levels = np.array([10, -10, 5, -5, 0])
    if k % 512:
        return np.exp2(np.random.permutation(np.resize(levels, k // 32))).repeat(32)
    a = np.empty((k // 512, 16))
    for p in range(k // 512):
        a[p, :8] = np.random.permutation(np.resize(levels, 8))
        for g in range(8):
            far = levels[np.abs(levels - a[p, g]) >= 10]
            a[p, g + 8] = far[np.random.randint(len(far))]
    return np.exp2(a.ravel()).repeat(32)


BF16 = ml_dtypes.bfloat16


def bf(x):
    return np.asarray(x, np.float32).astype(BF16)


def f64(x):
    return np.asarray(x).astype(np.float64)


N, K, D, F = 1024, 1024, 512, 1024


def sigmoid(a):
    return 0.5 * (1.0 + np.tanh(0.5 * a))


def draw0():
    s, v, u = mx_kscale(K), mx_kscale(D), mx_kscale(N)
    return {"x": bf(np.random.standard_normal((N, K)) * s * u[:, None]),
            "wm": bf(np.random.standard_normal((K, F)) / np.sqrt(K) / s[:, None]),
            "z": bf(np.random.standard_normal((N, D)) * v),
            "wg": bf(np.random.standard_normal((D, F)) / np.sqrt(D) / v[:, None]),
            "bg": bf(0.5 * np.random.standard_normal(F)),
            "bond": bf(2.0 * np.random.standard_normal((N, N)) / u),
            "edge": bf(np.random.standard_normal((N, N)) + 0.7 * np.random.standard_normal(N)[:, None]),
            "bo": bf(0.3 * np.random.standard_normal(F)),
            "h0": bf(0.5 * np.random.standard_normal((N, F)))}


def core(x, wm, z, wg, bg, bond, edge, bo, h0):
    c = mxq(f64(x), 1, "e4m3") @ mxq(f64(wm), 0, "e4m3")
    a = mxq(f64(z), 1, "e4m3") @ mxq(f64(wg), 0, "e4m3")
    m = c * sigmoid(a + f64(bg))
    e = sigmoid(f64(edge))
    mix = f64(bond) * e
    deg = np.sum(e, axis=1, keepdims=True)
    r = mxq(mix, 1, "e4m3") @ mxq(m, 0, "e4m3")
    y = r / np.sqrt(deg) + f64(bo)
    return f64(h0) + y * sigmoid(y)


def e4m3fn_bytes(y):
    return np.clip(np.asarray(y, np.float64), -448.0, 448.0).astype(np.float32).astype(ml_dtypes.float8_e4m3fn).view(np.uint8)


def e4m3fn_values(b):
    return np.asarray(b, np.uint8).view(ml_dtypes.float8_e4m3fn).astype(np.float64)


def setup_inputs():
    d = draw0()
    x0 = np.asarray(d['wm']).astype(np.float64)
    s = (np.max(np.abs(x0), axis=(1,), keepdims=True) / 448.0).astype(np.float32)
    out = {}
    for k, v in d.items():
        if k == 'wm':
            out['wm_bytes'] = e4m3fn_bytes(x0 / s.astype(np.float64))
            out['wm_scale'] = s
        else:
            out[k] = v
    return out


def reference(x, wm_bytes, wm_scale, z, wg, bg, bond, edge, bo, h0):
    return core(x, e4m3fn_values(wm_bytes) * wm_scale.astype(np.float64), z, wg, bg, bond, edge, bo, h0)

@@ -1,0 +1,261 @@
+from contextlib import ExitStack
+
+import concourse.mybir as mybir
+from concourse.masks import make_identity
+
+N, K, D, F = 1024, 1024, 512, 1024
+FLOPS = 2 * N * K * F + 2 * N * D * F + 2 * N * N * F
+F32 = mybir.dt.float32
+BF16 = mybir.dt.bfloat16
+U32 = mybir.dt.uint32
+U8 = mybir.dt.uint8
+FP8 = mybir.dt.float8_e4m3fn
+X4 = mybir.dt.float8_e4m3fn_x4
+ACT = mybir.ActivationFunctionType
+ALU = mybir.AluOpType
+
+ORDER = """small e,0 wm,0 wg,0 setup b,0 wm,1 x,0 z,0 e,1 b,1 x,1 e,2 b,2 wg,1 x,2 e,3 b,3 e,4 b,4 e,5 b,5 x,3 e,6 b,6 e,7 z,1 b,7 h,0 h,1 h,2 h,3 bgt se,0 bo,0 bo,1 ww,0,0,0 boc,0 ww,0,0,1 ww,0,0,2 boc,1 ww,0,0,3 wgi,0 wi,0,0 ww,0,1,0 ww,0,1,1 wgq,0 xT,0,0 ww,0,1,2 xT,0,1 wq,0,0 ww,0,1,3 zT,0 ww,1,0,0 xc,0,0 wi,0,1 xc,0,1 zT,1 zc,0 xq,0,0 zc,1 xq,0,1 xT,1,0 wq,0,1 se,1 xT,1,1 zq,0 zq,1 xc,1,0 ww,1,0,1 A,0,0 ww,1,0,2 xc,1,1 mm,0 sa,0,0 ww,1,1,0 xq,1,0 A,1,0 xq,1,1 xT,2,0 se,2 wgi,1 xT,2,1 C,0,0 sa,1,0 ww,1,0,3 C,1,0 xc,2,0 mg,0,0 A,2,0 xc,2,1 wgq,1 mT,0 sa,2,0 xq,2,0 C,2,0 xq,2,1 mc,0 mg,1,0 A,3,0 ww,1,1,1 mg,2,0 nT,0,0 sa,3,0 mq,0 xT,3,0 wi,1,0 nc,0,0 A,4,0 xT,3,1 xc,3,0 C,3,0 sa,4,0 nq,0,0 xq,3,0 xc,3,1 wq,1,0 A,5,0 zT,2 ww,1,1,2 mg,3,0 zT,3 sa,5,0 xq,3,1 nT,1,0 mm,1 zc,2 A,6,0 zc,3 C,0,1 zq,2 nc,1,0 C,1,1 zq,3 mm,2 sa,6,0 mT,1 se,3 A,0,1 nq,1,0 mT,2 sa,0,1 mm,3 mc,1 A,1,1 mc,2 mg,0,1 mT,3 sa,1,1 mq,1 C,2,1 mq,2 mc,3 mg,1,1 A,2,1 ww,1,1,3 mq,3 nT,0,1 sa,2,1 wi,1,1 C,3,1 se,4 A,3,1 mg,2,1 nc,0,1 wq,1,1 sa,3,1 nq,0,1 se,5 C,4,0 mg,3,1 A,4,1 mm,4 nT,1,1 sa,4,1 C,4,1 nc,1,1 mg,4,0 A,5,1 se,6 mT,4 mg,4,1 C,5,0 nq,1,1 mm,5 sa,5,1 C,5,1 mc,4 R,0,0 mg,5,0 se,7 A,6,1 mT,5 mq,4 mg,5,1 nT,2,0 sa,6,1 y,0,0 C,6,0 nc,2,0 mm,6 nT,2,1 mc,5 A,7,0 nc,2,1 C,6,1 nq,2,0 mq,5 sa,7,0 mT,6 nq,2,1 mg,6,0 R,0,1 mc,6 mg,6,1 A,7,1 C,7,0 sa,7,1 mq,6 y,0,1 C,7,1 si,0,0 mg,7,0 R,0,2 mg,7,1 nT,3,0 y,0,2 R,0,3 mm,7 nT,3,1 nc,3,0 R,0,4 nc,3,1 ad,0,0 mT,7 si,0,1 nq,3,0 nq,3,1 mc,7 adG,0,1 y,0,3 si,0,2 y,0,4 R,0,5 si,0,3 mq,7 ad,0,2 si,0,4 R,0,6 adG,0,3 y,0,5 y,0,6 R,0,7 si,0,5 ad,0,4 si,0,6 R,1,0 adG,0,5 y,0,7 y,1,0 R,1,1 si,0,7 ad,0,6 si,1,0 R,1,2 adG,0,7 y,1,1 y,1,2 R,1,3 si,1,1 ad,1,0 si,1,2 R,1,4 adG,1,1 y,1,3 y,1,4 R,1,5 si,1,3 ad,1,2 si,1,4 R,1,6 adG,1,3 y,1,5 y,1,6 R,1,7 si,1,5 ad,1,4 si,1,6 adG,1,5 y,1,7 si,1,7 ad,1,6 ad,1,7"""
+
+
+def tile_gated_edge_message_passing_f4_kernel(tc, x, wm_bytes, wm_scale, z, wg, bg, bond, edge, bo, h0, out):
+    nc = tc.nc
+    with ExitStack() as ctx:
+        keep = ctx.enter_context(tc.tile_pool(name="keep", bufs=1))
+        stage = ctx.enter_context(tc.tile_pool(name="stage", bufs=2))
+        psum = ctx.enter_context(tc.psum_pool(name="psum", bufs=2))
+        ctx.enter_context(tc.manual_schedule())
+
+        def kt(name, shape, dt):
+            return keep.tile(shape, dt, name=name, align_bytes=64)
+
+        zs = [kt("zs%d" % h, [128, 4, D], BF16) for h in range(2)]
+        wgs = [kt("wgs%d" % h, [128, 4, 512], BF16) for h in range(2)]
+        wmb = [kt("wmb%d" % g, [128, 4, F], U8) for g in range(2)]
+        xs = [kt("xs%d" % i, [128, 2, K], BF16) for i in range(4)]
+        bs = [kt("bs%d" % i, [128, N], BF16) for i in range(8)]
+        es = {}
+        hs = {}
+        zc, zsc = kt("zc", [128, N], U32), kt("zsc", [128, N], U8)
+        wgc, wgsc = kt("wgc", [128, F], U32), kt("wgsc", [128, F], U8)
+        xc, xsc = kt("xc", [128, 2, N], U32), kt("xsc", [128, 2, N], U8)
+        wc, wsc = kt("wc", [128, 2, F], U32), kt("wsc", [128, 2, F], U8)
+        mxc, mxsc = kt("mxc", [128, 8, 256], U32), kt("mxsc", [128, 8, 256], U8)
+        mc, msc = kt("mc", [128, 2, F], U32), kt("msc", [128, 2, F], U8)
+        gT = kt("gT", [128, 8, N], F32)
+        ident = kt("ident", [128, 128], F32)
+        identb = kt("identb", [128, 128], BF16)
+        ones = kt("ones", [128, 128], BF16)
+        borow = kt("borow", [128, F], BF16)
+        bob = kt("bob", [128, F], BF16)
+        bgrow = kt("bgrow", [128, 128], BF16)
+        bgc = kt("bgc", [128, 8], F32)
+        wms = kt("wms", [128, 2, 4], F32)
+        nhalf = kt("nhalf", [128, 1], F32)
+        warm = kt("warm", [128, 1], F32)
+        deg = [kt("deg%d" % i, [128, 8], F32) for i in range(8)]
+        rs = [kt("rs%d" % i, [128, 8], F32) for i in range(8)]
+        live = {}
+
+        def small():
+            nc.sync.dma_start(out=wms[:], in_=wm_scale.rearrange("(g p t) o -> p g (t o)", p=128, t=4))
+            nc.vector.memset(warm[:], 0.0)
+            nc.scalar.activation(out=warm[:], in_=warm[:], func=ACT.Sigmoid)
+            make_identity(nc, ident[:])
+            nc.vector.memset(bgrow[:], 0.0)
+            nc.vector.memset(borow[:], 0.0)
+            nc.vector.memset(ones[:], 1.0)
+            nc.vector.memset(nhalf[:], -0.5)
+            make_identity(nc, identb[:])
+
+        def setup():
+            nc.sync.dma_start(out=bgrow[0:8, :], in_=bg.rearrange("(j p) -> j p", p=128))
+            nc.sync.dma_start(out=borow[0:1, :], in_=bo.rearrange("(o f) -> o f", o=1))
+
+        def bgt():
+            bp = psum.tile([128, 128], BF16, tag="T", name="bp", bufs=3)
+            nc.tensor.transpose(bp[:], bgrow[:], identb[:])
+            nc.scalar.copy(out=bgc[:], in_=bp[:, 0:8])
+
+        def load(nm, i):
+            if nm == "z":
+                nc.sync.dma_start(out=zs[i][:], in_=z[i * 512:(i + 1) * 512, :].rearrange("(a p) k -> p a k", p=128))
+            elif nm == "wg":
+                nc.sync.dma_start(out=wgs[i][:], in_=wg[:, i * 512:(i + 1) * 512].rearrange("(p t) f -> p t f", t=4))
+            elif nm == "wm":
+                nc.sync.dma_start(out=wmb[i][:], in_=wm_bytes[i * 512:(i + 1) * 512, :].rearrange("(p t) f -> p t f", t=4))
+            elif nm == "x":
+                nc.sync.dma_start(out=xs[i][:], in_=x[i * 256:(i + 1) * 256, :].rearrange("(a p) k -> p a k", p=128))
+            elif nm == "e":
+                es[i] = stage.tile([128, N], BF16, tag="eh", name="es", bufs=8, align_bytes=64)
+                nc.sync.dma_start(out=es[i][:], in_=edge[i * 128:(i + 1) * 128, :])
+            elif nm == "b":
+                nc.sync.dma_start(out=bs[i][:], in_=bond[i * 128:(i + 1) * 128, :])
+            elif nm == "h":
+                for j in (2 * i, 2 * i + 1):
+                    hs[j] = stage.tile([128, F], BF16, tag="eh", name="hs", bufs=8, align_bytes=64)
+                    nc.sync.dma_start(out=hs[j][:], in_=h0[j * 128:(j + 1) * 128, :])
+
+        def words(ap, g, u):
+            return ap.bitcast(F32)[:, 256 * g + u:256 * (g + 1):2]
+
+        def bank(tag, bufs, key):
+            live[key] = psum.tile([128, 512], F32, tag=tag, name="bank" + tag, bufs=bufs)
+            return live[key]
+
+        def grp(key):
+            live[key] = stage.tile([128, 1024], BF16, tag="grp", name="grp", bufs=3, align_bytes=64)
+            return live[key]
+
+        def zT(pr):
+            b = bank("T", 3, "zT%d" % pr)[:].rearrange("p (u n) -> p u n", u=2)
+            for j in range(2):
+                for u in range(2):
+                    a = 2 * (pr % 2) + j
+                    nc.tensor.transpose(b[:, u, j * 128:(j + 1) * 128], words(zs[pr // 2][:, a, :], 0, u), ident[:])
+
+        def copyout(eng, key, src, pat):
+            g = grp(key)
+            o = g[:].bitcast(F32)
+            s = live[src][:].rearrange(*pat[0], **pat[1])
+            if eng == "S":
+                nc.scalar.copy(out=o.rearrange(*pat[2], **pat[3]), in_=s)
+            else:
+                nc.vector.tensor_copy(out=o.rearrange(*pat[2], **pat[3]), in_=s)
+
+        PAT2 = (("p (u n) -> p n u",), dict(u=2), ("p (n u) -> p n u",), dict(u=2))
+        PATM = (("p (g u n) -> p g n u",), dict(g=2, u=2), ("p (g n u) -> p g n u",), dict(g=2, u=2))
+
+        def quant(codes, scales, src):
+            nc.vector.quantize_mx(out=codes.bitcast(X4), scales=scales, in_=src)
+
+        def run(nm, i):
+            if nm in ("z", "wg", "wm", "x", "e", "b", "h"):
+                load(nm, i[0])
+            elif nm == "small":
+                small()
+            elif nm == "setup":
+                setup()
+            elif nm == "bgt":
+                bgt()
+            elif nm == "bo":
+                live["bo%d" % i[0]] = psum.tile([128, 512], F32, tag="T", name="bankbo", bufs=3)
+                nc.tensor.matmul(live["bo%d" % i[0]][:], lhsT=ones[:], rhs=borow[:, i[0] * 512:(i[0] + 1) * 512], start=True, stop=True)
+            elif nm == "boc":
+                nc.scalar.copy(out=bob[:, i[0] * 512:(i[0] + 1) * 512], in_=live["bo%d" % i[0]][:])
+            elif nm == "zT":
+                zT(i[0])
+            elif nm == "zc":
+                copyout("S", "zg%d" % i[0], "zT%d" % i[0], PAT2)
+            elif nm == "zq":
+                c = slice(i[0] * 256, (i[0] + 1) * 256)
+                quant(zc[:, c], zsc[:, c], live["zg%d" % i[0]][:])
+            elif nm == "wgi":
+                live["wgg%d" % i[0]] = stage.tile([128, 512, 4], BF16, tag="wgrp", name="wgg", bufs=2, align_bytes=64)
+                interleave(live["wgg%d" % i[0]], wgs[i[0]])
+            elif nm == "wgq":
+                c = slice(i[0] * 512, (i[0] + 1) * 512)
+                quant(wgc[:, c], wgsc[:, c], live["wgg%d" % i[0]][:].rearrange("p f t -> p (f t)"))
+            elif nm == "xT":
+                pr, g = i
+                b = bank("T", 3, "xT%d%d" % (pr, g))[:].rearrange("p (u n) -> p u n", u=2)
+                for j in range(2):
+                    for u in range(2):
+                        nc.tensor.transpose(b[:, u, j * 128:(j + 1) * 128], words(xs[pr][:, j, :], g, u), ident[:])
+            elif nm == "xc":
+                copyout("S", "xg%d%d" % (i[0], i[1]), "xT%d%d" % (i[0], i[1]), PAT2)
+            elif nm == "xq":
+                pr, g = i
+                c = slice(pr * 256, (pr + 1) * 256)
+                quant(xc[:, g, c], xsc[:, g, c], live["xg%d%d" % (pr, g)][:])
+            elif nm == "ww":
+                h, g, t = i
+                k = "ww%d%d" % (h, g)
+                if k not in live:
+                    live[k] = stage.tile([128, 4, 512], BF16, tag="wide", name="wide", bufs=2, align_bytes=64)
+                src = wmb[g][:, t, h * 512:(h + 1) * 512].bitcast(FP8)
+                if 4 * g + t < 4:
+                    nc.vector.tensor_scalar(out=live[k][:, t, :], in0=src, scalar1=wms[:, g, t:t + 1], scalar2=None, op0=ALU.mult)
+                else:
+                    nc.scalar.activation(out=live[k][:, t, :], in_=src, func=ACT.Copy, scale=wms[:, g, t:t + 1])
+            elif nm == "wi":
+                h, g = i
+                live["wi%d%d" % (h, g)] = stage.tile([128, 512, 4], BF16, tag="wgrp", name="wgg", bufs=2, align_bytes=64)
+                interleave(live["wi%d%d" % (h, g)], live["ww%d%d" % (h, g)])
+            elif nm == "wq":
+                h, g = i
+                c = slice(h * 512, (h + 1) * 512)
+                quant(wc[:, g, c], wsc[:, g, c], live["wi%d%d" % (h, g)][:].rearrange("p f t -> p (f t)"))
+            elif nm == "se":
+                live["e%d" % i[0]] = stage.tile([128, N], F32, tag="e32", name="e32", bufs=2, align_bytes=64)
+                nc.scalar.activation(out=live["e%d" % i[0]][:], in_=es[i[0]][:], func=ACT.Sigmoid, accum_out=deg[i[0]][:, 0:1])
+                nc.gpsimd.tensor_tensor(out=rs[i[0]][:, 0:1], in0=deg[i[0]][:, 0:1], in1=nhalf[:], op=ALU.pow)
+            elif nm == "mm":
+                live["mix%d" % i[0]] = stage.tile([128, N], BF16, tag="mix", name="mix", bufs=2, align_bytes=64)
+                nc.vector.tensor_tensor(out=live["mix%d" % i[0]][:], in0=bs[i[0]][:], in1=live["e%d" % i[0]][:], op=ALU.mult)
+            elif nm == "mT":
+                b = bank("T", 3, "mT%d" % i[0])[:].rearrange("p (g u n) -> p g u n", g=2, u=2)
+                for g in range(2):
+                    for u in range(2):
+                        nc.tensor.transpose(b[:, g, u, :], words(live["mix%d" % i[0]][:], g, u), ident[:])
+            elif nm == "mc":
+                copyout("S", "mg%d" % i[0], "mT%d" % i[0], PATM)
+            elif nm == "mq":
+                quant(mxc[:, i[0], :], mxsc[:, i[0], :], live["mg%d" % i[0]][:])
+            elif nm == "A":
+                f, nh = i
+                b = bank("A", 1, "A%d%d" % (f, nh))
+                fs, ns = slice(f * 128, (f + 1) * 128), slice(nh * 512, (nh + 1) * 512)
+                nc.tensor.matmul_mx(out=b[:], lhsT=wgc[:, fs].bitcast(X4), lhsT_scale=wgsc[:, fs], rhs=zc[:, ns].bitcast(X4), rhs_scale=zsc[:, ns], start=True, stop=True)
+            elif nm == "sa":
+                f, nh = i
+                nc.scalar.activation(out=gT[:, f, nh * 512:(nh + 1) * 512], in_=live["A%d%d" % (f, nh)][:], func=ACT.Sigmoid, bias=bgc[:, f:f + 1])
+            elif nm == "C":
+                f, nh = i
+                b = bank("C", 2, "C%d%d" % (f, nh))
+                fs, ns = slice(f * 128, (f + 1) * 128), slice(nh * 512, (nh + 1) * 512)
+                for g in range(2):
+                    nc.tensor.matmul_mx(out=b[:], lhsT=wc[:, g, fs].bitcast(X4), lhsT_scale=wsc[:, g, fs], rhs=xc[:, g, ns].bitcast(X4), rhs_scale=xsc[:, g, ns], start=(g == 0), stop=(g == 1))
+            elif nm == "mg":
+                f, nh = i
+                live["m%d%d" % (f, nh)] = stage.tile([128, 512], BF16, tag="mT", name="mTt", bufs=4, align_bytes=64)
+                nc.vector.tensor_tensor(out=live["m%d%d" % (f, nh)][:], in0=live["C%d%d" % (f, nh)][:], in1=gT[:, f, nh * 512:(nh + 1) * 512], op=ALU.mult)
+            elif nm == "nT":
+                fp, g = i
+                b = bank("T", 3, "nT%d%d" % (fp, g))[:].rearrange("p (u n) -> p u n", u=2)
+                for j in range(2):
+                    for u in range(2):
+                        nc.tensor.transpose(b[:, u, j * 128:(j + 1) * 128], words(live["m%d%d" % (2 * fp + j, g)][:], 0, u), ident[:])
+            elif nm == "nc":
+                copyout("S", "ng%d%d" % (i[0], i[1]), "nT%d%d" % (i[0], i[1]), PAT2)
+            elif nm == "nq":
+                fp, g = i
+                c = slice(fp * 256, (fp + 1) * 256)
+                quant(mc[:, g, c], msc[:, g, c], live["ng%d%d" % (fp, g)][:])
+            elif nm == "R":
+                h, t = i
+                b = bank("R", 2, "R%d%d" % (h, t))
+                fs = slice(h * 512, (h + 1) * 512)
+                for g in range(2):
+                    gs = slice(g * 128, (g + 1) * 128)
+                    nc.tensor.matmul_mx(out=b[:], lhsT=mxc[:, t, gs].bitcast(X4), lhsT_scale=mxsc[:, t, gs], rhs=mc[:, g, fs].bitcast(X4), rhs_scale=msc[:, g, fs], start=(g == 0), stop=(g == 1))
+            elif nm == "y":
+                h, t = i
+                live["y%d%d" % (h, t)] = stage.tile([128, 512], F32, tag="y", name="y", bufs=2, align_bytes=64)
+                nc.vector.scalar_tensor_tensor(out=live["y%d%d" % (h, t)][:], in0=live["R%d%d" % (h, t)][:], scalar=rs[t][:, 0:1], in1=bob[:, h * 512:(h + 1) * 512], op0=ALU.mult, op1=ALU.add)
+            elif nm == "si":
+                h, t = i
+                live["s%d%d" % (h, t)] = stage.tile([128, 512], F32, tag="s", name="s", bufs=2, align_bytes=64)
+                nc.scalar.activation(out=live["s%d%d" % (h, t)][:], in_=live["y%d%d" % (h, t)][:], func=ACT.Silu)
+            elif nm in ("ad", "adG"):
+                h, t = i
+                o = stage.tile([128, 512], F32, tag="o", name="o", bufs=4, align_bytes=64)
+                e = nc.gpsimd if nm == "adG" else nc.vector
+                e.tensor_tensor(out=o[:], in0=live["s%d%d" % (h, t)][:], in1=hs[t][:, h * 512:(h + 1) * 512], op=ALU.add)
+                nc.sync.dma_start(out=out[t * 128:(t + 1) * 128, h * 512:(h + 1) * 512], in_=o[:])
+
+        def interleave(dst, src):
+            nc.vector.tensor_copy(out=dst[:].rearrange("p (c i) t -> p c t i", i=4), in_=src[:].rearrange("p t (c i) -> p c t i", i=4))
+
+        for w in ORDER.split():
+            nm, *idx = w.split(",")
+            run(nm, [int(v) for v in idx])

@@ -14,7 +14,7 @@ X4 = mybir.dt.float8_e4m3fn_x4
 ACT = mybir.ActivationFunctionType
 ALU = mybir.AluOpType
 
-ORDER = """small e,0 wm,0 wg,0 setup b,0 wm,1 x,0 z,0 e,1 b,1 x,1 e,2 b,2 wg,1 x,2 e,3 b,3 e,4 b,4 e,5 b,5 x,3 e,6 b,6 e,7 z,1 b,7 h,0 h,1 h,2 h,3 bgt se,0 bo,0 bo,1 ww,0,0,0 boc,0 ww,0,0,1 ww,0,0,2 boc,1 ww,0,0,3 wgi,0 wi,0,0 ww,0,1,0 ww,0,1,1 wgq,0 xT,0,0 ww,0,1,2 xT,0,1 wq,0,0 ww,0,1,3 zT,0 ww,1,0,0 xc,0,0 wi,0,1 xc,0,1 zT,1 zc,0 xq,0,0 zc,1 xq,0,1 xT,1,0 wq,0,1 se,1 xT,1,1 zq,0 zq,1 xc,1,0 ww,1,0,1 A,0,0 ww,1,0,2 xc,1,1 mm,0 sa,0,0 ww,1,1,0 xq,1,0 A,1,0 xq,1,1 xT,2,0 se,2 wgi,1 xT,2,1 C,0,0 sa,1,0 ww,1,0,3 C,1,0 xc,2,0 mg,0,0 A,2,0 xc,2,1 wgq,1 mT,0 sa,2,0 xq,2,0 C,2,0 xq,2,1 mc,0 mg,1,0 A,3,0 ww,1,1,1 mg,2,0 nT,0,0 sa,3,0 mq,0 xT,3,0 wi,1,0 nc,0,0 A,4,0 xT,3,1 xc,3,0 C,3,0 sa,4,0 nq,0,0 xq,3,0 xc,3,1 wq,1,0 A,5,0 zT,2 ww,1,1,2 mg,3,0 zT,3 sa,5,0 xq,3,1 nT,1,0 mm,1 zc,2 A,6,0 zc,3 C,0,1 zq,2 nc,1,0 C,1,1 zq,3 mm,2 sa,6,0 mT,1 se,3 A,0,1 nq,1,0 mT,2 sa,0,1 mm,3 mc,1 A,1,1 mc,2 mg,0,1 mT,3 sa,1,1 mq,1 C,2,1 mq,2 mc,3 mg,1,1 A,2,1 ww,1,1,3 mq,3 nT,0,1 sa,2,1 wi,1,1 C,3,1 se,4 A,3,1 mg,2,1 nc,0,1 wq,1,1 sa,3,1 nq,0,1 se,5 C,4,0 mg,3,1 A,4,1 mm,4 nT,1,1 sa,4,1 C,4,1 nc,1,1 mg,4,0 A,5,1 se,6 mT,4 mg,4,1 C,5,0 nq,1,1 mm,5 sa,5,1 C,5,1 mc,4 R,0,0 mg,5,0 se,7 A,6,1 mT,5 mq,4 mg,5,1 nT,2,0 sa,6,1 y,0,0 C,6,0 nc,2,0 mm,6 nT,2,1 mc,5 A,7,0 nc,2,1 C,6,1 nq,2,0 mq,5 sa,7,0 mT,6 nq,2,1 mg,6,0 R,0,1 mc,6 mg,6,1 A,7,1 C,7,0 sa,7,1 mq,6 y,0,1 C,7,1 si,0,0 mg,7,0 R,0,2 mg,7,1 nT,3,0 y,0,2 R,0,3 mm,7 nT,3,1 nc,3,0 R,0,4 nc,3,1 ad,0,0 mT,7 si,0,1 nq,3,0 nq,3,1 mc,7 adG,0,1 y,0,3 si,0,2 y,0,4 R,0,5 si,0,3 mq,7 ad,0,2 si,0,4 R,0,6 adG,0,3 y,0,5 y,0,6 R,0,7 si,0,5 ad,0,4 si,0,6 R,1,0 adG,0,5 y,0,7 y,1,0 R,1,1 si,0,7 ad,0,6 si,1,0 R,1,2 adG,0,7 y,1,1 y,1,2 R,1,3 si,1,1 ad,1,0 si,1,2 R,1,4 adG,1,1 y,1,3 y,1,4 R,1,5 si,1,3 ad,1,2 si,1,4 R,1,6 adG,1,3 y,1,5 y,1,6 R,1,7 si,1,5 ad,1,4 si,1,6 adG,1,5 y,1,7 si,1,7 ad,1,6 ad,1,7"""
+ORDER = """small e,0 wm,0 wmx,0 setup x,0 b,0 ex,0 bx,0 x,1 z,0 e,1 wg,0 z,1 b,1 x,2 wm,1 e,2 x,3 b,2 e,3 b,3 h,0 h,1 h,2 h,3 boB bgt se,0 ww,0,0,0 ww,1,0,0 ww,0,0,1 ww,0,0,2 ww,0,0,3 ww,1,0,1 xT,0,0 ww,1,0,2 wi,0,0 ww,1,0,3 mm,0 xT,0,1 wi,1,0 mT,0 xc,0,0 wq,0,0 xc,0,1 xT,1,0 xq,0,0 mc,0 wq,1,0 se,1 zT,0 xq,0,1 mq,0 xT,1,1 xc,1,0 mm,1 zc,0 zT,1 se,2 xq,1,0 zq,0 mT,1 wgi,0 xc,1,1 zc,1 se,3 zT,2 xq,1,1 zq,1 wgq,0 mc,1 zT,3 mm,2 zc,2 A,0,0 mq,1 zc,3 zq,2 xT,2,0 mm,3 sa,0,0 xT,2,1 ww,0,1,0 xc,2,0 ww,1,1,0 zq,3 se,4 A,1,0 ww,0,1,1 xq,2,0 ww,0,1,2 A,0,1 ww,0,1,3 xc,2,1 ww,1,1,1 xT,3,0 ww,1,1,2 sa,1,0 ww,1,1,3 xq,2,1 sa,0,1 wi,0,1 A,1,1 se,5 A,2,0 xT,3,1 wi,1,1 A,2,1 xc,3,0 A,3,0 sa,1,1 mT,2 sa,2,0 mT,3 xq,3,0 wq,0,1 xc,3,1 A,3,1 wq,1,1 sa,2,1 C,0,0 xq,3,1 sa,3,0 wgi,1 mm,4 C,1,0 sa,3,1 C,0,1 mc,2 C,1,1 mg,0,0 mc,3 mg,0,1 se,6 mm,5 C,2,0 mg,1,0 mT,4 mg,1,1 se,7 nT,0,0 mg,2,0 nT,0,1 wgq,1 mc,4 C,2,1 mq,2 nc,0,0 mq,3 A,4,0 nc,0,1 mq,4 A,4,1 mg,2,1 A,5,0 sa,4,0 mT,5 nq,0,0 sa,4,1 nq,0,1 C,3,0 mm,6 sa,5,0 A,5,1 mc,5 R,0,0 mg,3,0 sa,5,1 A,6,0 mT,6 mm,7 sa,6,0 nT,1,0 mc,6 y,0,0 A,6,1 A,7,0 nc,1,0 mq,5 mT,7 mq,6 sa,6,1 C,3,1 nq,1,0 sa,7,0 A,7,1 mc,7 R,0,1 mg,3,1 sa,7,1 C,4,0 mq,7 y,0,1 nT,1,1 si,0,0 mg,4,0 R,0,2 C,4,1 y,0,2 R,0,3 mg,4,1 nc,1,1 C,5,0 ad,0,0 si,0,1 C,5,1 nq,1,1 si,0,2 C,6,0 y,0,3 adG,0,1 mg,5,0 si,0,3 R,1,0 mg,5,1 adG,0,2 nT,2,0 mg,6,0 nT,2,1 y,1,0 nc,2,0 R,1,1 ad,0,3 nc,2,1 C,6,1 nq,2,0 si,1,0 y,1,1 R,1,2 nq,2,1 C,7,0 mg,6,1 adG,1,0 si,1,1 R,1,3 y,1,2 C,7,1 adG,1,1 mg,7,0 si,1,2 R,2,0 y,1,3 nT,3,0 mg,7,1 adG,1,2 si,1,3 R,2,1 y,2,0 nc,3,0 nT,3,1 ad,1,3 si,2,0 R,2,2 nq,3,0 nc,3,1 y,2,1 R,2,3 adG,2,0 y,2,2 si,2,1 y,2,3 si,2,2 nq,3,1 adG,2,1 si,2,3 R,3,0 R,3,1 ad,2,2 R,3,2 adG,2,3 y,3,0 R,3,3 y,3,1 si,3,0 y,3,2 si,3,1 y,3,3 adG,3,0 si,3,2 si,3,3 ad,3,2 ad,3,3 adG,3,1"""
 
 
 def tile_gated_edge_message_passing_f4_kernel(tc, x, wm_bytes, wm_scale, z, wg, bg, bond, edge, bo, h0, out):
@@ -28,11 +28,11 @@ def tile_gated_edge_message_passing_f4_kernel(tc, x, wm_bytes, wm_scale, z, wg, 
         def kt(name, shape, dt):
             return keep.tile(shape, dt, name=name, align_bytes=64)
 
-        zs = [kt("zs%d" % h, [128, 4, D], BF16) for h in range(2)]
-        wgs = [kt("wgs%d" % h, [128, 4, 512], BF16) for h in range(2)]
+        zs = [kt("zs%d" % h, [128, 2, 2, D], BF16) for h in range(2)]
+        wgs = kt("wgs", [128, 4, F], BF16)
         wmb = [kt("wmb%d" % g, [128, 4, F], U8) for g in range(2)]
         xs = [kt("xs%d" % i, [128, 2, K], BF16) for i in range(4)]
-        bs = [kt("bs%d" % i, [128, N], BF16) for i in range(8)]
+        bs = [kt("bs%d" % i, [128, 2, N], BF16) for i in range(4)]
         es = {}
         hs = {}
         zc, zsc = kt("zc", [128, N], U32), kt("zsc", [128, N], U8)
@@ -44,8 +44,6 @@ def tile_gated_edge_message_passing_f4_kernel(tc, x, wm_bytes, wm_scale, z, wg, 
         gT = kt("gT", [128, 8, N], F32)
         ident = kt("ident", [128, 128], F32)
         identb = kt("identb", [128, 128], BF16)
-        ones = kt("ones", [128, 128], BF16)
-        borow = kt("borow", [128, F], BF16)
         bob = kt("bob", [128, F], BF16)
         bgrow = kt("bgrow", [128, 128], BF16)
         bgc = kt("bgc", [128, 8], F32)
@@ -62,38 +60,43 @@ def tile_gated_edge_message_passing_f4_kernel(tc, x, wm_bytes, wm_scale, z, wg, 
             nc.scalar.activation(out=warm[:], in_=warm[:], func=ACT.Sigmoid)
             make_identity(nc, ident[:])
             nc.vector.memset(bgrow[:], 0.0)
-            nc.vector.memset(borow[:], 0.0)
-            nc.vector.memset(ones[:], 1.0)
             nc.vector.memset(nhalf[:], -0.5)
             make_identity(nc, identb[:])
 
         def setup():
             nc.sync.dma_start(out=bgrow[0:8, :], in_=bg.rearrange("(j p) -> j p", p=128))
-            nc.sync.dma_start(out=borow[0:1, :], in_=bo.rearrange("(o f) -> o f", o=1))
 
         def bgt():
-            bp = psum.tile([128, 128], BF16, tag="T", name="bp", bufs=3)
+            bp = psum.tile([128, 128], BF16, tag="T", name="bp", bufs=4)
             nc.tensor.transpose(bp[:], bgrow[:], identb[:])
             nc.scalar.copy(out=bgc[:], in_=bp[:, 0:8])
 
         def load(nm, i):
             if nm == "z":
-                nc.sync.dma_start(out=zs[i][:], in_=z[i * 512:(i + 1) * 512, :].rearrange("(a p) k -> p a k", p=128))
+                nc.sync.dma_start(out=zs[i][:], in_=z[i * 512:(i + 1) * 512, :].rearrange("(q p a) k -> p q a k", p=128, a=2))
             elif nm == "wg":
-                nc.sync.dma_start(out=wgs[i][:], in_=wg[:, i * 512:(i + 1) * 512].rearrange("(p t) f -> p t f", t=4))
-            elif nm == "wm":
-                nc.sync.dma_start(out=wmb[i][:], in_=wm_bytes[i * 512:(i + 1) * 512, :].rearrange("(p t) f -> p t f", t=4))
+                nc.sync.dma_start(out=wgs[:], in_=wg.rearrange("(p t) f -> p t f", t=4))
+            elif nm in ("wm", "wmx"):
+                ts = slice(0, 4) if i else slice(2, 4) if nm == "wmx" else slice(0, 2)
+                nc.sync.dma_start(out=wmb[i][:, ts, :], in_=wm_bytes[i * 512:(i + 1) * 512, :].rearrange("(p t) f -> p t f", t=4)[:, ts, :])
+            elif nm == "boB":
+                nc.sync.dma_start(out=bob[:], in_=bo.partition_broadcast(128))
+            elif nm in ("ex", "bx") or (nm in "eb" and i == 0):
+                dst, src = (es, edge) if nm[0] == "e" else (bs, bond)
+                if nm == "e":
+                    es[0] = stage.tile([128, 2, N], BF16, tag="eh", name="es", bufs=4, align_bytes=64)
+                a = len(nm) - 1
+                nc.sync.dma_start(out=dst[0][:, a, :], in_=src[0:256, :].rearrange("(p a) n -> p a n", a=2)[:, a, :])
             elif nm == "x":
-                nc.sync.dma_start(out=xs[i][:], in_=x[i * 256:(i + 1) * 256, :].rearrange("(a p) k -> p a k", p=128))
+                nc.sync.dma_start(out=xs[i][:], in_=x[i * 256:(i + 1) * 256, :].rearrange("(p a) k -> p a k", a=2))
             elif nm == "e":
-                es[i] = stage.tile([128, N], BF16, tag="eh", name="es", bufs=8, align_bytes=64)
-                nc.sync.dma_start(out=es[i][:], in_=edge[i * 128:(i + 1) * 128, :])
+                es[i] = stage.tile([128, 2, N], BF16, tag="eh", name="es", bufs=4, align_bytes=64)
+                nc.sync.dma_start(out=es[i][:], in_=edge[i * 256:(i + 1) * 256, :].rearrange("(p a) n -> p a n", a=2))
             elif nm == "b":
-                nc.sync.dma_start(out=bs[i][:], in_=bond[i * 128:(i + 1) * 128, :])
+                nc.sync.dma_start(out=bs[i][:], in_=bond[i * 256:(i + 1) * 256, :].rearrange("(p a) n -> p a n", a=2))
             elif nm == "h":
-                for j in (2 * i, 2 * i + 1):
-                    hs[j] = stage.tile([128, F], BF16, tag="eh", name="hs", bufs=8, align_bytes=64)
-                    nc.sync.dma_start(out=hs[j][:], in_=h0[j * 128:(j + 1) * 128, :])
+                hs[i] = stage.tile([128, 2, F], BF16, tag="eh", name="hs", bufs=4, align_bytes=64)
+                nc.sync.dma_start(out=hs[i][:], in_=h0[i * 256:(i + 1) * 256, :].rearrange("(p a) f -> p a f", a=2))
 
         def words(ap, g, u):
             return ap.bitcast(F32)[:, 256 * g + u:256 * (g + 1):2]
@@ -103,15 +106,14 @@ def tile_gated_edge_message_passing_f4_kernel(tc, x, wm_bytes, wm_scale, z, wg, 
             return live[key]
 
         def grp(key):
-            live[key] = stage.tile([128, 1024], BF16, tag="grp", name="grp", bufs=3, align_bytes=64)
+            live[key] = stage.tile([128, 1024], BF16, tag="grp", name="grp", bufs=5, align_bytes=64)
             return live[key]
 
         def zT(pr):
-            b = bank("T", 3, "zT%d" % pr)[:].rearrange("p (u n) -> p u n", u=2)
+            b = bank("T", 4, "zT%d" % pr)[:].rearrange("p (u n) -> p u n", u=2)
             for j in range(2):
                 for u in range(2):
-                    a = 2 * (pr % 2) + j
-                    nc.tensor.transpose(b[:, u, j * 128:(j + 1) * 128], words(zs[pr // 2][:, a, :], 0, u), ident[:])
+                    nc.tensor.transpose(b[:, u, j * 128:(j + 1) * 128], words(zs[pr // 2][:, pr % 2, j, :], 0, u), ident[:])
 
         def copyout(eng, key, src, pat):
             g = grp(key)
@@ -123,46 +125,45 @@ def tile_gated_edge_message_passing_f4_kernel(tc, x, wm_bytes, wm_scale, z, wg, 
                 nc.vector.tensor_copy(out=o.rearrange(*pat[2], **pat[3]), in_=s)
 
         PAT2 = (("p (u n) -> p n u",), dict(u=2), ("p (n u) -> p n u",), dict(u=2))
+        PATX = (("p (u a n) -> p n a u",), dict(u=2, a=2), ("p (n a u) -> p n a u",), dict(u=2, a=2))
+        VC = []
+        MG = ['mm4', 'mm5']
+        IS = ['wi00']
         PATM = (("p (g u n) -> p g n u",), dict(g=2, u=2), ("p (g n u) -> p g n u",), dict(g=2, u=2))
 
         def quant(codes, scales, src):
             nc.vector.quantize_mx(out=codes.bitcast(X4), scales=scales, in_=src)
 
         def run(nm, i):
-            if nm in ("z", "wg", "wm", "x", "e", "b", "h"):
-                load(nm, i[0])
+            if nm in ("z", "wg", "wm", "wmx", "ex", "bx", "boB", "x", "e", "b", "h"):
+                load(nm, i[0] if i else 0)
             elif nm == "small":
                 small()
             elif nm == "setup":
                 setup()
             elif nm == "bgt":
                 bgt()
-            elif nm == "bo":
-                live["bo%d" % i[0]] = psum.tile([128, 512], F32, tag="T", name="bankbo", bufs=3)
-                nc.tensor.matmul(live["bo%d" % i[0]][:], lhsT=ones[:], rhs=borow[:, i[0] * 512:(i[0] + 1) * 512], start=True, stop=True)
-            elif nm == "boc":
-                nc.scalar.copy(out=bob[:, i[0] * 512:(i[0] + 1) * 512], in_=live["bo%d" % i[0]][:])
             elif nm == "zT":
                 zT(i[0])
             elif nm == "zc":
-                copyout("S", "zg%d" % i[0], "zT%d" % i[0], PAT2)
+                copyout("V" if "zc%d" % i[0] in VC else "S", "zg%d" % i[0], "zT%d" % i[0], PATX)
             elif nm == "zq":
                 c = slice(i[0] * 256, (i[0] + 1) * 256)
                 quant(zc[:, c], zsc[:, c], live["zg%d" % i[0]][:])
             elif nm == "wgi":
                 live["wgg%d" % i[0]] = stage.tile([128, 512, 4], BF16, tag="wgrp", name="wgg", bufs=2, align_bytes=64)
-                interleave(live["wgg%d" % i[0]], wgs[i[0]])
+                interleave("wgi%d" % i[0], live["wgg%d" % i[0]], wgs[:, :, i[0] * 512:(i[0] + 1) * 512])
             elif nm == "wgq":
                 c = slice(i[0] * 512, (i[0] + 1) * 512)
                 quant(wgc[:, c], wgsc[:, c], live["wgg%d" % i[0]][:].rearrange("p f t -> p (f t)"))
             elif nm == "xT":
                 pr, g = i
-                b = bank("T", 3, "xT%d%d" % (pr, g))[:].rearrange("p (u n) -> p u n", u=2)
+                b = bank("T", 4, "xT%d%d" % (pr, g))[:].rearrange("p (u n) -> p u n", u=2)
                 for j in range(2):
                     for u in range(2):
                         nc.tensor.transpose(b[:, u, j * 128:(j + 1) * 128], words(xs[pr][:, j, :], g, u), ident[:])
             elif nm == "xc":
-                copyout("S", "xg%d%d" % (i[0], i[1]), "xT%d%d" % (i[0], i[1]), PAT2)
+                copyout("V" if "xc%d%d" % (i[0], i[1]) in VC else "S", "xg%d%d" % (i[0], i[1]), "xT%d%d" % (i[0], i[1]), PATX)
             elif nm == "xq":
                 pr, g = i
                 c = slice(pr * 256, (pr + 1) * 256)
@@ -173,37 +174,37 @@ def tile_gated_edge_message_passing_f4_kernel(tc, x, wm_bytes, wm_scale, z, wg, 
                 if k not in live:
                     live[k] = stage.tile([128, 4, 512], BF16, tag="wide", name="wide", bufs=2, align_bytes=64)
                 src = wmb[g][:, t, h * 512:(h + 1) * 512].bitcast(FP8)
-                if 4 * g + t < 4:
+                if 4 * g + t < 8:
                     nc.vector.tensor_scalar(out=live[k][:, t, :], in0=src, scalar1=wms[:, g, t:t + 1], scalar2=None, op0=ALU.mult)
                 else:
                     nc.scalar.activation(out=live[k][:, t, :], in_=src, func=ACT.Copy, scale=wms[:, g, t:t + 1])
             elif nm == "wi":
                 h, g = i
                 live["wi%d%d" % (h, g)] = stage.tile([128, 512, 4], BF16, tag="wgrp", name="wgg", bufs=2, align_bytes=64)
-                interleave(live["wi%d%d" % (h, g)], live["ww%d%d" % (h, g)])
+                interleave("wi%d%d" % (h, g), live["wi%d%d" % (h, g)], live["ww%d%d" % (h, g)][:])
             elif nm == "wq":
                 h, g = i
                 c = slice(h * 512, (h + 1) * 512)
                 quant(wc[:, g, c], wsc[:, g, c], live["wi%d%d" % (h, g)][:].rearrange("p f t -> p (f t)"))
             elif nm == "se":
-                live["e%d" % i[0]] = stage.tile([128, N], F32, tag="e32", name="e32", bufs=2, align_bytes=64)
-                nc.scalar.activation(out=live["e%d" % i[0]][:], in_=es[i[0]][:], func=ACT.Sigmoid, accum_out=deg[i[0]][:, 0:1])
+                live["e%d" % i[0]] = stage.tile([128, N], F32, tag="e32", name="e32", bufs=3, align_bytes=64)
+                nc.scalar.activation(out=live["e%d" % i[0]][:], in_=es[i[0] // 2][:, i[0] % 2, :], func=ACT.Sigmoid, accum_out=deg[i[0]][:, 0:1])
                 nc.gpsimd.tensor_tensor(out=rs[i[0]][:, 0:1], in0=deg[i[0]][:, 0:1], in1=nhalf[:], op=ALU.pow)
             elif nm == "mm":
-                live["mix%d" % i[0]] = stage.tile([128, N], BF16, tag="mix", name="mix", bufs=2, align_bytes=64)
-                nc.vector.tensor_tensor(out=live["mix%d" % i[0]][:], in0=bs[i[0]][:], in1=live["e%d" % i[0]][:], op=ALU.mult)
+                live["mix%d" % i[0]] = stage.tile([128, N], BF16, tag="mix", name="mix", bufs=3, align_bytes=64)
+                (nc.gpsimd if "mm%d" % i[0] in MG else nc.vector).tensor_tensor(out=live["mix%d" % i[0]][:], in0=bs[i[0] // 2][:, i[0] % 2, :], in1=live["e%d" % i[0]][:], op=ALU.mult)
             elif nm == "mT":
-                b = bank("T", 3, "mT%d" % i[0])[:].rearrange("p (g u n) -> p g u n", g=2, u=2)
+                b = bank("T", 4, "mT%d" % i[0])[:].rearrange("p (g u n) -> p g u n", g=2, u=2)
                 for g in range(2):
                     for u in range(2):
                         nc.tensor.transpose(b[:, g, u, :], words(live["mix%d" % i[0]][:], g, u), ident[:])
             elif nm == "mc":
-                copyout("S", "mg%d" % i[0], "mT%d" % i[0], PATM)
+                copyout("V" if "mc%d" % i[0] in VC else "S", "mg%d" % i[0], "mT%d" % i[0], PATM)
             elif nm == "mq":
                 quant(mxc[:, i[0], :], mxsc[:, i[0], :], live["mg%d" % i[0]][:])
             elif nm == "A":
                 f, nh = i
-                b = bank("A", 1, "A%d%d" % (f, nh))
+                b = bank("X", 4, "A%d%d" % (f, nh))
                 fs, ns = slice(f * 128, (f + 1) * 128), slice(nh * 512, (nh + 1) * 512)
                 nc.tensor.matmul_mx(out=b[:], lhsT=wgc[:, fs].bitcast(X4), lhsT_scale=wgsc[:, fs], rhs=zc[:, ns].bitcast(X4), rhs_scale=zsc[:, ns], start=True, stop=True)
             elif nm == "sa":
@@ -211,50 +212,58 @@ def tile_gated_edge_message_passing_f4_kernel(tc, x, wm_bytes, wm_scale, z, wg, 
                 nc.scalar.activation(out=gT[:, f, nh * 512:(nh + 1) * 512], in_=live["A%d%d" % (f, nh)][:], func=ACT.Sigmoid, bias=bgc[:, f:f + 1])
             elif nm == "C":
                 f, nh = i
-                b = bank("C", 2, "C%d%d" % (f, nh))
+                b = bank("X", 4, "C%d%d" % (f, nh))
                 fs, ns = slice(f * 128, (f + 1) * 128), slice(nh * 512, (nh + 1) * 512)
                 for g in range(2):
                     nc.tensor.matmul_mx(out=b[:], lhsT=wc[:, g, fs].bitcast(X4), lhsT_scale=wsc[:, g, fs], rhs=xc[:, g, ns].bitcast(X4), rhs_scale=xsc[:, g, ns], start=(g == 0), stop=(g == 1))
             elif nm == "mg":
                 f, nh = i
-                live["m%d%d" % (f, nh)] = stage.tile([128, 512], BF16, tag="mT", name="mTt", bufs=4, align_bytes=64)
+                live["m%d%d" % (f, nh)] = stage.tile([128, 512], BF16, tag="mT", name="mTt", bufs=6, align_bytes=64)
                 nc.vector.tensor_tensor(out=live["m%d%d" % (f, nh)][:], in0=live["C%d%d" % (f, nh)][:], in1=gT[:, f, nh * 512:(nh + 1) * 512], op=ALU.mult)
             elif nm == "nT":
                 fp, g = i
-                b = bank("T", 3, "nT%d%d" % (fp, g))[:].rearrange("p (u n) -> p u n", u=2)
+                b = bank("T", 4, "nT%d%d" % (fp, g))[:].rearrange("p (u n) -> p u n", u=2)
                 for j in range(2):
                     for u in range(2):
                         nc.tensor.transpose(b[:, u, j * 128:(j + 1) * 128], words(live["m%d%d" % (2 * fp + j, g)][:], 0, u), ident[:])
             elif nm == "nc":
-                copyout("S", "ng%d%d" % (i[0], i[1]), "nT%d%d" % (i[0], i[1]), PAT2)
+                copyout("V" if "nc%d%d" % (i[0], i[1]) in VC else "S", "ng%d%d" % (i[0], i[1]), "nT%d%d" % (i[0], i[1]), PAT2)
             elif nm == "nq":
                 fp, g = i
                 c = slice(fp * 256, (fp + 1) * 256)
                 quant(mc[:, g, c], msc[:, g, c], live["ng%d%d" % (fp, g)][:])
             elif nm == "R":
-                h, t = i
-                b = bank("R", 2, "R%d%d" % (h, t))
-                fs = slice(h * 512, (h + 1) * 512)
-                for g in range(2):
-                    gs = slice(g * 128, (g + 1) * 128)
-                    nc.tensor.matmul_mx(out=b[:], lhsT=mxc[:, t, gs].bitcast(X4), lhsT_scale=mxsc[:, t, gs], rhs=mc[:, g, fs].bitcast(X4), rhs_scale=msc[:, g, fs], start=(g == 0), stop=(g == 1))
+                q, t = i
+                b = bank("X", 4, "R%d%d" % (q, t))
+                fs = slice(q * 256, (q + 1) * 256)
+                for a in range(2):
+                    for g in range(2):
+                        gs = slice(g * 128, (g + 1) * 128)
+                        nc.tensor.matmul_mx(out=b[:, a * 256:(a + 1) * 256], lhsT=mxc[:, 2 * t + a, gs].bitcast(X4), lhsT_scale=mxsc[:, 2 * t + a, gs], rhs=mc[:, g, fs].bitcast(X4), rhs_scale=msc[:, g, fs], start=(g == 0), stop=(g == 1))
             elif nm == "y":
-                h, t = i
-                live["y%d%d" % (h, t)] = stage.tile([128, 512], F32, tag="y", name="y", bufs=2, align_bytes=64)
-                nc.vector.scalar_tensor_tensor(out=live["y%d%d" % (h, t)][:], in0=live["R%d%d" % (h, t)][:], scalar=rs[t][:, 0:1], in1=bob[:, h * 512:(h + 1) * 512], op0=ALU.mult, op1=ALU.add)
+                q, t = i
+                live["y%d%d" % (q, t)] = stage.tile([128, 512], F32, tag="y", name="y", bufs=4, align_bytes=64)
+                for a in range(2):
+                    cs = slice(a * 256, (a + 1) * 256)
+                    nc.vector.scalar_tensor_tensor(out=live["y%d%d" % (q, t)][:, cs], in0=live["R%d%d" % (q, t)][:, cs], scalar=rs[2 * t + a][:, 0:1], in1=bob[:, q * 256:(q + 1) * 256], op0=ALU.mult, op1=ALU.add)
             elif nm == "si":
-                h, t = i
-                live["s%d%d" % (h, t)] = stage.tile([128, 512], F32, tag="s", name="s", bufs=2, align_bytes=64)
-                nc.scalar.activation(out=live["s%d%d" % (h, t)][:], in_=live["y%d%d" % (h, t)][:], func=ACT.Silu)
+                q, t = i
+                live["s%d%d" % (q, t)] = stage.tile([128, 512], F32, tag="s", name="s", bufs=4, align_bytes=64)
+                nc.scalar.activation(out=live["s%d%d" % (q, t)][:], in_=live["y%d%d" % (q, t)][:], func=ACT.Silu)
             elif nm in ("ad", "adG"):
-                h, t = i
-                o = stage.tile([128, 512], F32, tag="o", name="o", bufs=4, align_bytes=64)
+                q, t = i
+                o = stage.tile([128, 2, 256], F32, tag="o", name="o", bufs=4, align_bytes=64)
                 e = nc.gpsimd if nm == "adG" else nc.vector
-                e.tensor_tensor(out=o[:], in0=live["s%d%d" % (h, t)][:], in1=hs[t][:, h * 512:(h + 1) * 512], op=ALU.add)
-                nc.sync.dma_start(out=out[t * 128:(t + 1) * 128, h * 512:(h + 1) * 512], in_=o[:])
+                fs = slice(q * 256, (q + 1) * 256)
+                e.tensor_tensor(out=o[:], in0=live["s%d%d" % (q, t)][:].rearrange("p (a f) -> p a f", a=2), in1=hs[t][:, :, fs], op=ALU.add)
+                nc.sync.dma_start(out=out.rearrange("(b p a) f -> b p a f", p=128, a=2)[t, :, :, fs], in_=o[:])
 
-        def interleave(dst, src):
-            nc.vector.tensor_copy(out=dst[:].rearrange("p (c i) t -> p c t i", i=4), in_=src[:].rearrange("p t (c i) -> p c t i", i=4))
+        def interleave(key, dst, src):
+            dv, sv = dst[:].rearrange("p (c i) t -> p c t i", i=4), src.rearrange("p t (c i) -> p c t i", i=4)
+            if key in IS:
+                nc.scalar.copy(out=dv, in_=sv)
+            else:
+                nc.vector.tensor_copy(out=dv, in_=sv)
 
         for w in ORDER.split():
             nm, *idx = w.split(",")

from contextlib import ExitStack

import concourse.mybir as mybir
from concourse.masks import make_identity

N, K, D, F = 1024, 1024, 512, 1024
FLOPS = 2 * N * K * F + 2 * N * D * F + 2 * N * N * F
F32 = mybir.dt.float32
BF16 = mybir.dt.bfloat16
U32 = mybir.dt.uint32
U8 = mybir.dt.uint8
FP8 = mybir.dt.float8_e4m3fn
X4 = mybir.dt.float8_e4m3fn_x4
ACT = mybir.ActivationFunctionType
ALU = mybir.AluOpType

ORDER = """small e,0 wm,0 wmx,0 setup x,0 b,0 ex,0 bx,0 x,1 z,0 e,1 wg,0 z,1 b,1 x,2 wm,1 e,2 x,3 b,2 e,3 b,3 h,0 h,1 h,2 h,3 boB bgt se,0 ww,0,0,0 ww,1,0,0 ww,0,0,1 ww,0,0,2 ww,0,0,3 ww,1,0,1 xT,0,0 ww,1,0,2 wi,0,0 ww,1,0,3 mm,0 xT,0,1 wi,1,0 mT,0 xc,0,0 wq,0,0 xc,0,1 xT,1,0 xq,0,0 mc,0 wq,1,0 se,1 zT,0 xq,0,1 mq,0 xT,1,1 xc,1,0 mm,1 zc,0 zT,1 se,2 xq,1,0 zq,0 mT,1 wgi,0 xc,1,1 zc,1 se,3 zT,2 xq,1,1 zq,1 wgq,0 mc,1 zT,3 mm,2 zc,2 A,0,0 mq,1 zc,3 zq,2 xT,2,0 mm,3 sa,0,0 xT,2,1 ww,0,1,0 xc,2,0 ww,1,1,0 zq,3 se,4 A,1,0 ww,0,1,1 xq,2,0 ww,0,1,2 A,0,1 ww,0,1,3 xc,2,1 ww,1,1,1 xT,3,0 ww,1,1,2 sa,1,0 ww,1,1,3 xq,2,1 sa,0,1 wi,0,1 A,1,1 se,5 A,2,0 xT,3,1 wi,1,1 A,2,1 xc,3,0 A,3,0 sa,1,1 mT,2 sa,2,0 mT,3 xq,3,0 wq,0,1 xc,3,1 A,3,1 wq,1,1 sa,2,1 C,0,0 xq,3,1 sa,3,0 wgi,1 mm,4 C,1,0 sa,3,1 C,0,1 mc,2 C,1,1 mg,0,0 mc,3 mg,0,1 se,6 mm,5 C,2,0 mg,1,0 mT,4 mg,1,1 se,7 nT,0,0 mg,2,0 nT,0,1 wgq,1 mc,4 C,2,1 mq,2 nc,0,0 mq,3 A,4,0 nc,0,1 mq,4 A,4,1 mg,2,1 A,5,0 sa,4,0 mT,5 nq,0,0 sa,4,1 nq,0,1 C,3,0 mm,6 sa,5,0 A,5,1 mc,5 R,0,0 mg,3,0 sa,5,1 A,6,0 mT,6 mm,7 sa,6,0 nT,1,0 mc,6 y,0,0 A,6,1 A,7,0 nc,1,0 mq,5 mT,7 mq,6 sa,6,1 C,3,1 nq,1,0 sa,7,0 A,7,1 mc,7 R,0,1 mg,3,1 sa,7,1 C,4,0 mq,7 y,0,1 nT,1,1 si,0,0 mg,4,0 R,0,2 C,4,1 y,0,2 R,0,3 mg,4,1 nc,1,1 C,5,0 ad,0,0 si,0,1 C,5,1 nq,1,1 si,0,2 C,6,0 y,0,3 adG,0,1 mg,5,0 si,0,3 R,1,0 mg,5,1 adG,0,2 nT,2,0 mg,6,0 nT,2,1 y,1,0 nc,2,0 R,1,1 ad,0,3 nc,2,1 C,6,1 nq,2,0 si,1,0 y,1,1 R,1,2 nq,2,1 C,7,0 mg,6,1 adG,1,0 si,1,1 R,1,3 y,1,2 C,7,1 adG,1,1 mg,7,0 si,1,2 R,2,0 y,1,3 nT,3,0 mg,7,1 adG,1,2 si,1,3 R,2,1 y,2,0 nc,3,0 nT,3,1 ad,1,3 si,2,0 R,2,2 nq,3,0 nc,3,1 y,2,1 R,2,3 adG,2,0 y,2,2 si,2,1 y,2,3 si,2,2 nq,3,1 adG,2,1 si,2,3 R,3,0 R,3,1 ad,2,2 R,3,2 adG,2,3 y,3,0 R,3,3 y,3,1 si,3,0 y,3,2 si,3,1 y,3,3 adG,3,0 si,3,2 si,3,3 ad,3,2 ad,3,3 adG,3,1"""


def tile_gated_edge_message_passing_f4_kernel(tc, x, wm_bytes, wm_scale, z, wg, bg, bond, edge, bo, h0, out):
    nc = tc.nc
    with ExitStack() as ctx:
        keep = ctx.enter_context(tc.tile_pool(name="keep", bufs=1))
        stage = ctx.enter_context(tc.tile_pool(name="stage", bufs=2))
        psum = ctx.enter_context(tc.psum_pool(name="psum", bufs=2))
        ctx.enter_context(tc.manual_schedule())

        def kt(name, shape, dt):
            return keep.tile(shape, dt, name=name, align_bytes=64)

        zs = [kt("zs%d" % h, [128, 2, 2, D], BF16) for h in range(2)]
        wgs = kt("wgs", [128, 4, F], BF16)
        wmb = [kt("wmb%d" % g, [128, 4, F], U8) for g in range(2)]
        xs = [kt("xs%d" % i, [128, 2, K], BF16) for i in range(4)]
        bs = [kt("bs%d" % i, [128, 2, N], BF16) for i in range(4)]
        es = {}
        hs = {}
        zc, zsc = kt("zc", [128, N], U32), kt("zsc", [128, N], U8)
        wgc, wgsc = kt("wgc", [128, F], U32), kt("wgsc", [128, F], U8)
        xc, xsc = kt("xc", [128, 2, N], U32), kt("xsc", [128, 2, N], U8)
        wc, wsc = kt("wc", [128, 2, F], U32), kt("wsc", [128, 2, F], U8)
        mxc, mxsc = kt("mxc", [128, 8, 256], U32), kt("mxsc", [128, 8, 256], U8)
        mc, msc = kt("mc", [128, 2, F], U32), kt("msc", [128, 2, F], U8)
        gT = kt("gT", [128, 8, N], F32)
        ident = kt("ident", [128, 128], F32)
        identb = kt("identb", [128, 128], BF16)
        bob = kt("bob", [128, F], BF16)
        bgrow = kt("bgrow", [128, 128], BF16)
        bgc = kt("bgc", [128, 8], F32)
        wms = kt("wms", [128, 2, 4], F32)
        nhalf = kt("nhalf", [128, 1], F32)
        warm = kt("warm", [128, 1], F32)
        deg = [kt("deg%d" % i, [128, 8], F32) for i in range(8)]
        rs = [kt("rs%d" % i, [128, 8], F32) for i in range(8)]
        live = {}

        def small():
            nc.sync.dma_start(out=wms[:], in_=wm_scale.rearrange("(g p t) o -> p g (t o)", p=128, t=4))
            nc.vector.memset(warm[:], 0.0)
            nc.scalar.activation(out=warm[:], in_=warm[:], func=ACT.Sigmoid)
            make_identity(nc, ident[:])
            nc.vector.memset(bgrow[:], 0.0)
            nc.vector.memset(nhalf[:], -0.5)
            make_identity(nc, identb[:])

        def setup():
            nc.sync.dma_start(out=bgrow[0:8, :], in_=bg.rearrange("(j p) -> j p", p=128))

        def bgt():
            bp = psum.tile([128, 128], BF16, tag="T", name="bp", bufs=4)
            nc.tensor.transpose(bp[:], bgrow[:], identb[:])
            nc.scalar.copy(out=bgc[:], in_=bp[:, 0:8])

        def load(nm, i):
            if nm == "z":
                nc.sync.dma_start(out=zs[i][:], in_=z[i * 512:(i + 1) * 512, :].rearrange("(q p a) k -> p q a k", p=128, a=2))
            elif nm == "wg":
                nc.sync.dma_start(out=wgs[:], in_=wg.rearrange("(p t) f -> p t f", t=4))
            elif nm in ("wm", "wmx"):
                ts = slice(0, 4) if i else slice(2, 4) if nm == "wmx" else slice(0, 2)
                nc.sync.dma_start(out=wmb[i][:, ts, :], in_=wm_bytes[i * 512:(i + 1) * 512, :].rearrange("(p t) f -> p t f", t=4)[:, ts, :])
            elif nm == "boB":
                nc.sync.dma_start(out=bob[:], in_=bo.partition_broadcast(128))
            elif nm in ("ex", "bx") or (nm in "eb" and i == 0):
                dst, src = (es, edge) if nm[0] == "e" else (bs, bond)
                if nm == "e":
                    es[0] = stage.tile([128, 2, N], BF16, tag="eh", name="es", bufs=4, align_bytes=64)
                a = len(nm) - 1
                nc.sync.dma_start(out=dst[0][:, a, :], in_=src[0:256, :].rearrange("(p a) n -> p a n", a=2)[:, a, :])
            elif nm == "x":
                nc.sync.dma_start(out=xs[i][:], in_=x[i * 256:(i + 1) * 256, :].rearrange("(p a) k -> p a k", a=2))
            elif nm == "e":
                es[i] = stage.tile([128, 2, N], BF16, tag="eh", name="es", bufs=4, align_bytes=64)
                nc.sync.dma_start(out=es[i][:], in_=edge[i * 256:(i + 1) * 256, :].rearrange("(p a) n -> p a n", a=2))
            elif nm == "b":
                nc.sync.dma_start(out=bs[i][:], in_=bond[i * 256:(i + 1) * 256, :].rearrange("(p a) n -> p a n", a=2))
            elif nm == "h":
                hs[i] = stage.tile([128, 2, F], BF16, tag="eh", name="hs", bufs=4, align_bytes=64)
                nc.sync.dma_start(out=hs[i][:], in_=h0[i * 256:(i + 1) * 256, :].rearrange("(p a) f -> p a f", a=2))

        def words(ap, g, u):
            return ap.bitcast(F32)[:, 256 * g + u:256 * (g + 1):2]

        def bank(tag, bufs, key):
            live[key] = psum.tile([128, 512], F32, tag=tag, name="bank" + tag, bufs=bufs)
            return live[key]

        def grp(key):
            live[key] = stage.tile([128, 1024], BF16, tag="grp", name="grp", bufs=5, align_bytes=64)
            return live[key]

        def zT(pr):
            b = bank("T", 4, "zT%d" % pr)[:].rearrange("p (u n) -> p u n", u=2)
            for j in range(2):
                for u in range(2):
                    nc.tensor.transpose(b[:, u, j * 128:(j + 1) * 128], words(zs[pr // 2][:, pr % 2, j, :], 0, u), ident[:])

        def copyout(eng, key, src, pat):
            g = grp(key)
            o = g[:].bitcast(F32)
            s = live[src][:].rearrange(*pat[0], **pat[1])
            if eng == "S":
                nc.scalar.copy(out=o.rearrange(*pat[2], **pat[3]), in_=s)
            else:
                nc.vector.tensor_copy(out=o.rearrange(*pat[2], **pat[3]), in_=s)

        PAT2 = (("p (u n) -> p n u",), dict(u=2), ("p (n u) -> p n u",), dict(u=2))
        PATX = (("p (u a n) -> p n a u",), dict(u=2, a=2), ("p (n a u) -> p n a u",), dict(u=2, a=2))
        VC = []
        MG = ['mm4', 'mm5']
        IS = ['wi00']
        PATM = (("p (g u n) -> p g n u",), dict(g=2, u=2), ("p (g n u) -> p g n u",), dict(g=2, u=2))

        def quant(codes, scales, src):
            nc.vector.quantize_mx(out=codes.bitcast(X4), scales=scales, in_=src)

        def run(nm, i):
            if nm in ("z", "wg", "wm", "wmx", "ex", "bx", "boB", "x", "e", "b", "h"):
                load(nm, i[0] if i else 0)
            elif nm == "small":
                small()
            elif nm == "setup":
                setup()
            elif nm == "bgt":
                bgt()
            elif nm == "zT":
                zT(i[0])
            elif nm == "zc":
                copyout("V" if "zc%d" % i[0] in VC else "S", "zg%d" % i[0], "zT%d" % i[0], PATX)
            elif nm == "zq":
                c = slice(i[0] * 256, (i[0] + 1) * 256)
                quant(zc[:, c], zsc[:, c], live["zg%d" % i[0]][:])
            elif nm == "wgi":
                live["wgg%d" % i[0]] = stage.tile([128, 512, 4], BF16, tag="wgrp", name="wgg", bufs=2, align_bytes=64)
                interleave("wgi%d" % i[0], live["wgg%d" % i[0]], wgs[:, :, i[0] * 512:(i[0] + 1) * 512])
            elif nm == "wgq":
                c = slice(i[0] * 512, (i[0] + 1) * 512)
                quant(wgc[:, c], wgsc[:, c], live["wgg%d" % i[0]][:].rearrange("p f t -> p (f t)"))
            elif nm == "xT":
                pr, g = i
                b = bank("T", 4, "xT%d%d" % (pr, g))[:].rearrange("p (u n) -> p u n", u=2)
                for j in range(2):
                    for u in range(2):
                        nc.tensor.transpose(b[:, u, j * 128:(j + 1) * 128], words(xs[pr][:, j, :], g, u), ident[:])
            elif nm == "xc":
                copyout("V" if "xc%d%d" % (i[0], i[1]) in VC else "S", "xg%d%d" % (i[0], i[1]), "xT%d%d" % (i[0], i[1]), PATX)
            elif nm == "xq":
                pr, g = i
                c = slice(pr * 256, (pr + 1) * 256)
                quant(xc[:, g, c], xsc[:, g, c], live["xg%d%d" % (pr, g)][:])
            elif nm == "ww":
                h, g, t = i
                k = "ww%d%d" % (h, g)
                if k not in live:
                    live[k] = stage.tile([128, 4, 512], BF16, tag="wide", name="wide", bufs=2, align_bytes=64)
                src = wmb[g][:, t, h * 512:(h + 1) * 512].bitcast(FP8)
                if 4 * g + t < 8:
                    nc.vector.tensor_scalar(out=live[k][:, t, :], in0=src, scalar1=wms[:, g, t:t + 1], scalar2=None, op0=ALU.mult)
                else:
                    nc.scalar.activation(out=live[k][:, t, :], in_=src, func=ACT.Copy, scale=wms[:, g, t:t + 1])
            elif nm == "wi":
                h, g = i
                live["wi%d%d" % (h, g)] = stage.tile([128, 512, 4], BF16, tag="wgrp", name="wgg", bufs=2, align_bytes=64)
                interleave("wi%d%d" % (h, g), live["wi%d%d" % (h, g)], live["ww%d%d" % (h, g)][:])
            elif nm == "wq":
                h, g = i
                c = slice(h * 512, (h + 1) * 512)
                quant(wc[:, g, c], wsc[:, g, c], live["wi%d%d" % (h, g)][:].rearrange("p f t -> p (f t)"))
            elif nm == "se":
                live["e%d" % i[0]] = stage.tile([128, N], F32, tag="e32", name="e32", bufs=3, align_bytes=64)
                nc.scalar.activation(out=live["e%d" % i[0]][:], in_=es[i[0] // 2][:, i[0] % 2, :], func=ACT.Sigmoid, accum_out=deg[i[0]][:, 0:1])
                nc.gpsimd.tensor_tensor(out=rs[i[0]][:, 0:1], in0=deg[i[0]][:, 0:1], in1=nhalf[:], op=ALU.pow)
            elif nm == "mm":
                live["mix%d" % i[0]] = stage.tile([128, N], BF16, tag="mix", name="mix", bufs=3, align_bytes=64)
                (nc.gpsimd if "mm%d" % i[0] in MG else nc.vector).tensor_tensor(out=live["mix%d" % i[0]][:], in0=bs[i[0] // 2][:, i[0] % 2, :], in1=live["e%d" % i[0]][:], op=ALU.mult)
            elif nm == "mT":
                b = bank("T", 4, "mT%d" % i[0])[:].rearrange("p (g u n) -> p g u n", g=2, u=2)
                for g in range(2):
                    for u in range(2):
                        nc.tensor.transpose(b[:, g, u, :], words(live["mix%d" % i[0]][:], g, u), ident[:])
            elif nm == "mc":
                copyout("V" if "mc%d" % i[0] in VC else "S", "mg%d" % i[0], "mT%d" % i[0], PATM)
            elif nm == "mq":
                quant(mxc[:, i[0], :], mxsc[:, i[0], :], live["mg%d" % i[0]][:])
            elif nm == "A":
                f, nh = i
                b = bank("X", 4, "A%d%d" % (f, nh))
                fs, ns = slice(f * 128, (f + 1) * 128), slice(nh * 512, (nh + 1) * 512)
                nc.tensor.matmul_mx(out=b[:], lhsT=wgc[:, fs].bitcast(X4), lhsT_scale=wgsc[:, fs], rhs=zc[:, ns].bitcast(X4), rhs_scale=zsc[:, ns], start=True, stop=True)
            elif nm == "sa":
                f, nh = i
                nc.scalar.activation(out=gT[:, f, nh * 512:(nh + 1) * 512], in_=live["A%d%d" % (f, nh)][:], func=ACT.Sigmoid, bias=bgc[:, f:f + 1])
            elif nm == "C":
                f, nh = i
                b = bank("X", 4, "C%d%d" % (f, nh))
                fs, ns = slice(f * 128, (f + 1) * 128), slice(nh * 512, (nh + 1) * 512)
                for g in range(2):
                    nc.tensor.matmul_mx(out=b[:], lhsT=wc[:, g, fs].bitcast(X4), lhsT_scale=wsc[:, g, fs], rhs=xc[:, g, ns].bitcast(X4), rhs_scale=xsc[:, g, ns], start=(g == 0), stop=(g == 1))
            elif nm == "mg":
                f, nh = i
                live["m%d%d" % (f, nh)] = stage.tile([128, 512], BF16, tag="mT", name="mTt", bufs=6, align_bytes=64)
                nc.vector.tensor_tensor(out=live["m%d%d" % (f, nh)][:], in0=live["C%d%d" % (f, nh)][:], in1=gT[:, f, nh * 512:(nh + 1) * 512], op=ALU.mult)
            elif nm == "nT":
                fp, g = i
                b = bank("T", 4, "nT%d%d" % (fp, g))[:].rearrange("p (u n) -> p u n", u=2)
                for j in range(2):
                    for u in range(2):
                        nc.tensor.transpose(b[:, u, j * 128:(j + 1) * 128], words(live["m%d%d" % (2 * fp + j, g)][:], 0, u), ident[:])
            elif nm == "nc":
                copyout("V" if "nc%d%d" % (i[0], i[1]) in VC else "S", "ng%d%d" % (i[0], i[1]), "nT%d%d" % (i[0], i[1]), PAT2)
            elif nm == "nq":
                fp, g = i
                c = slice(fp * 256, (fp + 1) * 256)
                quant(mc[:, g, c], msc[:, g, c], live["ng%d%d" % (fp, g)][:])
            elif nm == "R":
                q, t = i
                b = bank("X", 4, "R%d%d" % (q, t))
                fs = slice(q * 256, (q + 1) * 256)
                for a in range(2):
                    for g in range(2):
                        gs = slice(g * 128, (g + 1) * 128)
                        nc.tensor.matmul_mx(out=b[:, a * 256:(a + 1) * 256], lhsT=mxc[:, 2 * t + a, gs].bitcast(X4), lhsT_scale=mxsc[:, 2 * t + a, gs], rhs=mc[:, g, fs].bitcast(X4), rhs_scale=msc[:, g, fs], start=(g == 0), stop=(g == 1))
            elif nm == "y":
                q, t = i
                live["y%d%d" % (q, t)] = stage.tile([128, 512], F32, tag="y", name="y", bufs=4, align_bytes=64)
                for a in range(2):
                    cs = slice(a * 256, (a + 1) * 256)
                    nc.vector.scalar_tensor_tensor(out=live["y%d%d" % (q, t)][:, cs], in0=live["R%d%d" % (q, t)][:, cs], scalar=rs[2 * t + a][:, 0:1], in1=bob[:, q * 256:(q + 1) * 256], op0=ALU.mult, op1=ALU.add)
            elif nm == "si":
                q, t = i
                live["s%d%d" % (q, t)] = stage.tile([128, 512], F32, tag="s", name="s", bufs=4, align_bytes=64)
                nc.scalar.activation(out=live["s%d%d" % (q, t)][:], in_=live["y%d%d" % (q, t)][:], func=ACT.Silu)
            elif nm in ("ad", "adG"):
                q, t = i
                o = stage.tile([128, 2, 256], F32, tag="o", name="o", bufs=4, align_bytes=64)
                e = nc.gpsimd if nm == "adG" else nc.vector
                fs = slice(q * 256, (q + 1) * 256)
                e.tensor_tensor(out=o[:], in0=live["s%d%d" % (q, t)][:].rearrange("p (a f) -> p a f", a=2), in1=hs[t][:, :, fs], op=ALU.add)
                nc.sync.dma_start(out=out.rearrange("(b p a) f -> b p a f", p=128, a=2)[t, :, :, fs], in_=o[:])

        def interleave(key, dst, src):
            dv, sv = dst[:].rearrange("p (c i) t -> p c t i", i=4), src.rearrange("p t (c i) -> p c t i", i=4)
            if key in IS:
                nc.scalar.copy(out=dv, in_=sv)
            else:
                nc.vector.tensor_copy(out=dv, in_=sv)

        for w in ORDER.split():
            nm, *idx = w.split(",")
            run(nm, [int(v) for v in idx])
